import numpy as np
import ml_dtypes


def mxq(x, axis, fmt="e4m3"):
    dtype, down = {"e4m3": (ml_dtypes.float8_e4m3fn, 7), "e5m2": (ml_dtypes.float8_e5m2, 14)}[fmt]
    v = np.moveaxis(np.asarray(x, np.float32).astype(ml_dtypes.bfloat16).astype(np.float64), axis, -1)
    blocks = v.reshape(v.shape[:-1] + (-1, 32))
    amax = np.abs(blocks).max(-1, keepdims=True)
    byte = np.maximum(np.where(amax > 0, np.frexp(amax)[1] - 1 + 127, 0) - down, 1)
    scale = np.exp2(byte - 127.0)
    codes = (blocks / scale).astype(np.float32).astype(dtype).astype(np.float64)
    return np.moveaxis((codes * scale).reshape(v.shape), -1, axis)


WIDE = False


def mx_kscale(k):
    if not WIDE:
        return np.ones(k)
    levels = np.array([10, -10, 5, -5, 0])
    if k % 512:
        return np.exp2(np.random.permutation(np.resize(levels, k // 32))).repeat(32)
    a = np.empty((k // 512, 16))
    for p in range(k // 512):
        a[p, :8] = np.random.permutation(np.resize(levels, 8))
        for g in range(8):
            far = levels[np.abs(levels - a[p, g]) >= 10]
            a[p, g + 8] = far[np.random.randint(len(far))]
    return np.exp2(a.ravel()).repeat(32)


BF16 = ml_dtypes.bfloat16


def bf(x):
    return np.asarray(x, np.float32).astype(BF16)


def f64(x):
    return np.asarray(x).astype(np.float64)


E2M1 = np.array([0.0, 0.5, 1.0, 1.5, 2.0, 3.0, 4.0, 6.0, -0.0, -0.5, -1.0, -1.5, -2.0, -3.0, -4.0, -6.0])


def pack_weight(w, fmt):
    k, n = w.shape
    w = f64(bf(w)).reshape(k // 32, 32, n)
    amax = np.abs(w).max(1)
    if fmt == "e4m3":
        byte = np.frexp(amax)[1] - 1 + 127 - 7
    else:
        mant, ex = np.frexp(amax / 6.0)
        byte = np.where(mant > 0.5, ex, ex - 1) + 127
    byte = np.clip(np.where(amax > 0, byte, 1), 1, 254)
    scaled = (w * np.exp2(127.0 - byte)[:, None, :]).reshape(k, n).astype(np.float32)
    by_word = np.ascontiguousarray(scaled.reshape(k // 512, 128, 4, n).transpose(0, 1, 3, 2))
    if fmt == "e4m3":
        words = by_word.astype(ml_dtypes.float8_e4m3fn).view(np.uint8)
    else:
        c = by_word.astype(ml_dtypes.float4_e2m1fn).view(np.uint8) & 0xF
        words = c[..., 0::2] | (c[..., 1::2] << 4)
    return np.ascontiguousarray(words), np.ascontiguousarray(byte.astype(np.uint8).reshape(k // 512, 16, n))


def unpack_weight(words, scales, fmt):
    g, p, n, _ = words.shape
    if fmt == "e4m3":
        vals = np.ascontiguousarray(words).view(ml_dtypes.float8_e4m3fn).astype(np.float64)
    else:
        nib = np.empty((g, p, n, 4), np.uint8)
        nib[..., 0::2] = words & 0xF
        nib[..., 1::2] = words >> 4
        vals = E2M1[nib]
    vals = vals * np.repeat(np.exp2(scales.astype(np.float64) - 127.0), 8, axis=1)[..., None]
    return vals.transpose(0, 1, 3, 2).reshape(g * 512, n)
def pack4(w):
    words, scales = pack_weight(w, "e2m1")
    return words.reshape(words.shape[0], 128, -1), scales


def unpack4(words, scales):
    return unpack_weight(words.reshape(words.shape[0], 128, -1, 2), scales, "e2m1")


N, R = 1536, 512


def draw0():
    s, u, t = mx_kscale(N), mx_kscale(N), mx_kscale(R)
    hop = np.random.standard_normal((N, N)) / np.sqrt(N) * s
    left = np.random.standard_normal((N, R)) / R ** 0.25 / s[:, None] * t
    right = np.random.standard_normal((R, N)) / R ** 0.25 / t[:, None] * u
    hinv = np.random.standard_normal((N, N)) / np.sqrt(N) / u[:, None]
    hinv_words, hinv_scales = pack4(hinv)
    return {"hop": bf(hop),
            "left": bf(left),
            "right": bf(right),
            "hinv_words": hinv_words,
            "hinv_scales": hinv_scales,
            "field": bf(0.5 * np.random.standard_normal(N))}


def core(hop, left, right, hinv_words, hinv_scales, field):
    w = np.exp(f64(field))
    a = (mxq(f64(hop), 1, "e4m3") @ mxq(f64(left), 0, "e4m3")) * w[:, None]
    c = (mxq(f64(right), 1, "e4m3") @ unpack4(hinv_words, hinv_scales)) / w
    return mxq(a, 1, "e4m3") @ mxq(c, 0, "e4m3")


def e4m3fn_bytes(y):
    return np.clip(np.asarray(y, np.float64), -448.0, 448.0).astype(np.float32).astype(ml_dtypes.float8_e4m3fn).view(np.uint8)


def e4m3fn_values(b):
    return np.asarray(b, np.uint8).view(ml_dtypes.float8_e4m3fn).astype(np.float64)


def setup_inputs():
    d = draw0()
    x0 = np.asarray(d['hop']).astype(np.float64)
    s = (np.max(np.abs(x0), axis=(0,), keepdims=True) / 448.0).astype(np.float32)
    out = {}
    for k, v in d.items():
        if k == 'hop':
            out['hop_bytes'] = e4m3fn_bytes(x0 / s.astype(np.float64))
            out['hop_scale'] = s
        else:
            out[k] = v
    return out


def reference(hop_bytes, hop_scale, left, right, hinv_words, hinv_scales, field):
    return core(e4m3fn_values(hop_bytes) * hop_scale.astype(np.float64), left, right, hinv_words, hinv_scales, field)

@@ -1,0 +1,311 @@
+from contextlib import ExitStack
+
+import concourse.mybir as mybir
+from concourse.masks import make_identity
+
+SITES, ORB = 1536, 512
+
+F32 = mybir.dt.float32
+BF16 = mybir.dt.bfloat16
+U32 = mybir.dt.uint32
+I32 = mybir.dt.int32
+U8 = mybir.dt.uint8
+FP8 = mybir.dt.float8_e4m3fn
+E4M3X4 = mybir.dt.float8_e4m3fn_x4
+E2M1X4 = mybir.dt.float4_e2m1fn_x4
+MULT = mybir.AluOpType.mult
+EXP = mybir.ActivationFunctionType.Exp
+
+P = 128
+PACK = 4
+K_PASS = P * PACK
+PASSES = SITES // K_PASS
+PAIRS = SITES // (2 * P)
+TILES = SITES // P
+N_OUT = 512
+
+FLOPS = 3 * 2 * SITES * SITES * ORB
+
+
+def tile_wrap_occupied_green_s11_kernel(tc, hop_bytes, hop_scale, left, right, hinv_words, hinv_scales, field, out):
+    nc = tc.nc
+
+    with ExitStack() as ctx:
+        keep = ctx.enter_context(tc.tile_pool(name="keep", bufs=1))
+        work = ctx.enter_context(tc.tile_pool(name="work", bufs=2))
+        results = ctx.enter_context(tc.tile_pool(name="results", bufs=6))
+        psum = ctx.enter_context(tc.psum_pool(name="psum", bufs=1))
+
+        ident = keep.tile([P, P], F32)
+        warm = keep.tile([P, 1], F32)
+        scale_bc = keep.tile([P, SITES], F32)
+        field_bc = keep.tile([P, SITES], BF16)
+        w_bc = keep.tile([P, SITES], F32)
+        winv_bc = keep.tile([P, SITES], F32)
+        right_rows = keep.tile([P, PACK, SITES], BF16)
+        hinv_codes = keep.tile([P, PASSES, 2 * SITES], U8, align_bytes=64)
+        hinv_sc = keep.tile([P, PASSES, SITES], U8, align_bytes=64)
+        right_codes = keep.tile([P, 2, PASSES, 2 * P], U32, align_bytes=64)
+        right_sc = keep.tile([P, 2, PASSES, 2 * P], U8, align_bytes=64)
+        left_codes = keep.tile([P, PASSES, ORB], U32, align_bytes=64)
+        left_sc = keep.tile([P, PASSES, ORB], U8, align_bytes=64)
+        c_codes = keep.tile([P, SITES], U32, align_bytes=64)
+        c_sc = keep.tile([P, SITES], U8, align_bytes=64)
+
+        hop_raw, left_rows = {}, {}
+        hop_view = hop_bytes.rearrange("(c p s) k -> c p s k", p=P, s=2)
+        left_view = left.rearrange("(g p j) r -> g p j r", p=P, j=PACK)
+        right_view = right.rearrange("(m t) k -> m t k", t=PACK)
+        out_view = out.rearrange("(c p s) j -> c p s j", p=P, s=2)
+
+        def load_hop(c):
+            hop_tile = keep.tile([P, 2, SITES], U8, name=f"hop_raw{c}")
+            nc.sync.dma_start(out=hop_tile[:], in_=hop_view[c])
+            hop_raw[c] = hop_tile
+
+        def load_scale(g):
+            k = slice(K_PASS * g, K_PASS * (g + 1))
+            nc.sync.dma_start(out=scale_bc[:, k], in_=hop_scale[:, k].rearrange("o k -> (o k)").partition_broadcast(P))
+
+        def load_left(g):
+            left_tile = keep.tile([P, PACK, ORB], BF16, name=f"left_rows{g}")
+            nc.sync.dma_start(out=left_tile[:], in_=left_view[g])
+            left_rows[g] = left_tile
+
+        def load_right(h):
+            nc.sync.dma_start(out=right_rows[:, 2 * h : 2 * h + 2, :], in_=right_view[:, 2 * h : 2 * h + 2, :])
+
+        hop_bf, hop_grouped, hop_codes, hop_sc = {}, {}, {}, {}
+
+        def widen(i, g0=0, g1=PASSES):
+            if g0 == 0:
+                bf_tile = work.tile([P, SITES], BF16, name="hop_bf", bufs=3)
+                hop_bf[i] = bf_tile
+            k = slice(K_PASS * g0, K_PASS * g1)
+            nc.vector.tensor_tensor(out=hop_bf[i][:, k], in0=hop_raw[i // 2][:, i % 2, k].bitcast(FP8), in1=scale_bc[:, k], op=MULT)
+
+        def turn(rows_of_slot, grouped, slots, copy):
+            for b in range(0, slots, 2):
+                n = min(2, slots - b)
+                bank = psum.tile([P, 2, 2, P], F32, name="turned", bufs=3)
+                for l in range(n):
+                    words = rows_of_slot(b + l)
+                    for u in range(2):
+                        nc.tensor.transpose(bank[:, l, u, :], words[:, u : 2 * P : 2], ident[:])
+                copy(
+                    out=grouped[:, b : b + n, :].bitcast(F32).rearrange("p l (r u) -> p l r u", u=2),
+                    in_=bank[:, 0:n, :, :].rearrange("p l u r -> p l r u"),
+                )
+
+        def turn_hop(i):
+            grouped = work.tile([P, PASSES, K_PASS], BF16, name="hop_grouped", align_bytes=64, bufs=3)
+            hop_grouped[i] = grouped
+            turn(lambda g: hop_bf[i][:, K_PASS * g : K_PASS * (g + 1)].bitcast(F32), grouped, PASSES, S)
+
+        def quantize_slots(grouped, codes, sc, spans):
+            flat = grouped[:].rearrange("p l k -> p (l k)")
+            for a, b in spans:
+                nc.vector.quantize_mx(out=codes[:, a // 4 : b // 4].bitcast(E4M3X4), scales=sc[:, a // 4 : b // 4], in_=flat[:, a:b])
+
+        def quantize_hop(i):
+            code_tile = keep.tile([P, PASSES * P], U32, name=f"hop_codes{i}", align_bytes=64)
+            sc_tile = keep.tile([P, PASSES * P], U8, name=f"hop_sc{i}", align_bytes=64)
+            hop_codes[i], hop_sc[i] = code_tile, sc_tile
+            quantize_slots(hop_grouped[i], code_tile, sc_tile, ((0, 1024), (1024, 1536)))
+
+        right_grouped = {}
+
+        def turn_right(h):
+            grouped = work.tile([P, 2 * PASSES, K_PASS], BF16, name="right_grouped", align_bytes=64)
+            right_grouped[h] = grouped
+            turn(lambda i: right_rows[:, 2 * h + i % 2, K_PASS * (i // 2) : K_PASS * (i // 2 + 1)].bitcast(F32), grouped, 2 * PASSES, S)
+
+        def quantize_right(h):
+            quantize_slots(
+                right_grouped[h],
+                right_codes[:, h, :, :].rearrange("p g m -> p (g m)"),
+                right_sc[:, h, :, :].rearrange("p g m -> p (g m)"),
+                ((0, 2048), (2048, 3072)),
+            )
+
+        def load_hinv(h):
+            cols = slice(SITES * h, SITES * (h + 1))
+            nc.sync.dma_start(out=hinv_codes[:, :, cols], in_=hinv_words[:, :, cols].rearrange("g p n -> p g n"))
+
+        left_grouped = {}
+
+        def interleave_left(g, engine_copy):
+            grouped = work.tile([P, ORB * PACK], BF16, name="left_grouped", align_bytes=64)
+            left_grouped[g] = grouped
+            engine_copy(
+                out=grouped[:].rearrange("p (t m j) -> p t m j", t=PACK, j=PACK),
+                in_=left_rows[g][:].rearrange("p j (m t) -> p t m j", t=PACK),
+            )
+
+        def quantize_left(g):
+            nc.vector.quantize_mx(out=left_codes[:, g, :].bitcast(E4M3X4), scales=left_sc[:, g, :], in_=left_grouped[g][:])
+
+        c_acc, c_grouped, a_acc, a_grouped, a_codes, a_sc = {}, {}, {}, {}, {}, {}
+
+        def mult_c(n):
+            acc = psum.tile([P, PACK, P], F32, name="acc", bufs=2)
+            c_acc[n] = acc
+            for t in range(PACK):
+                for g in range(PASSES):
+                    m = P * (t % 2)
+                    nc.tensor.matmul_mx(
+                        out=acc[:, t, :],
+                        lhsT=right_codes[:, t // 2, g, m : m + P].bitcast(E4M3X4),
+                        lhsT_scale=right_sc[:, t // 2, g, m : m + P],
+                        rhs=hinv_codes[:, g, 2 * P * n : 2 * P * (n + 1)].bitcast(E2M1X4),
+                        rhs_scale=hinv_sc[:, g, P * n : P * (n + 1)],
+                        start=(g == 0),
+                        stop=(g == PASSES - 1),
+                    )
+
+        def empty_c(n):
+            if n % 2 == 0:
+                grouped = work.tile([P, 2, P, PACK], BF16, name="c_grouped", align_bytes=64)
+                c_grouped[n // 2] = grouped
+            nc.vector.tensor_tensor(
+                out=c_grouped[n // 2][:, n % 2, :, :],
+                in0=c_acc[n][:].rearrange("p t n -> p n t"),
+                in1=winv_bc[:, P * n : P * (n + 1)].unsqueeze(2).to_broadcast([P, P, PACK]),
+                op=MULT,
+            )
+
+        def quantize_c(q):
+            cols = slice(2 * P * q, 2 * P * (q + 1))
+            nc.vector.quantize_mx(
+                out=c_codes[:, cols].bitcast(E4M3X4),
+                scales=c_sc[:, cols],
+                in_=c_grouped[q][:].rearrange("p s n t -> p (s n t)"),
+            )
+
+        def mult_a(i):
+            acc = psum.tile([P, PACK, P], F32, name="acc", bufs=2)
+            a_acc[i] = acc
+            for t in range(PACK):
+                for g in range(PASSES):
+                    cols = slice(g * P, (g + 1) * P)
+                    nc.tensor.matmul_mx(
+                        out=acc[:, t, :],
+                        lhsT=left_codes[:, g, P * t : P * (t + 1)].bitcast(E4M3X4),
+                        lhsT_scale=left_sc[:, g, P * t : P * (t + 1)],
+                        rhs=hop_codes[i][:, cols].bitcast(E4M3X4),
+                        rhs_scale=hop_sc[i][:, cols],
+                        start=(g == 0),
+                        stop=(g == PASSES - 1),
+                    )
+
+        def empty_a(i):
+            grouped = work.tile([P, P, PACK], BF16, name="a_grouped", align_bytes=64, bufs=3)
+            a_grouped[i] = grouped
+            w0 = 2 * P * (i // 2) + i % 2
+            nc.vector.tensor_tensor(
+                out=grouped[:],
+                in0=a_acc[i][:].rearrange("p t n -> p n t"),
+                in1=w_bc[:, w0 : w0 + 2 * P - 1 : 2].unsqueeze(2).to_broadcast([P, P, PACK]),
+                op=MULT,
+            )
+
+        def quantize_a(i):
+            code_tile = work.tile([P, P], U32, name="a_codes", align_bytes=64, bufs=3)
+            sc_tile = work.tile([P, P], U8, name="a_sc", align_bytes=64, bufs=3)
+            a_codes[i], a_sc[i] = code_tile, sc_tile
+            nc.vector.quantize_mx(out=code_tile[:].bitcast(E4M3X4), scales=sc_tile[:], in_=a_grouped[i][:].rearrange("p n t -> p (n t)"))
+
+        def finish(i, copies):
+            result = results.tile([P, SITES], F32, name="result")
+            for q in range(SITES // N_OUT):
+                cols = slice(N_OUT * q, N_OUT * (q + 1))
+                bank = psum.tile([P, N_OUT], F32, name="res", bufs=3)
+                nc.tensor.matmul_mx(
+                    out=bank[:],
+                    lhsT=a_codes[i][:].bitcast(E4M3X4),
+                    lhsT_scale=a_sc[i][:],
+                    rhs=c_codes[:, cols].bitcast(E4M3X4),
+                    rhs_scale=c_sc[:, cols],
+                    start=True,
+                    stop=True,
+                )
+                copies[q](out=result[:, cols], in_=bank[:])
+            nc.sync.dma_start(out=out_view[i // 2, :, i % 2, :], in_=result[:])
+
+        S = nc.scalar.copy
+        V = nc.vector.tensor_copy
+
+        with tc.manual_schedule():
+            nc.gpsimd.memset(warm[:], 0.0)
+            nc.gpsimd.memset(hinv_sc[:].rearrange("p g n -> p (g n)").bitcast(U32), 0)
+            make_identity(nc, ident[:])
+            load_scale(0)
+            load_hop(0)
+            load_scale(1)
+            load_scale(2)
+            load_right(0)
+            load_hop(1)
+            load_right(1)
+            for q in range(4):
+                nc.sync.dma_start(
+                    out=hinv_sc[32 * q : 32 * q + 4, :, :].bitcast(I32),
+                    in_=hinv_scales[:, 4 * q : 4 * q + 4, :].rearrange("g q n -> q g n").bitcast(I32),
+                )
+            nc.sync.dma_start(out=field_bc[:], in_=field.partition_broadcast(P))
+            load_hinv(0)
+            load_left(0)
+            load_hinv(1)
+            load_left(1)
+            load_left(2)
+            load_hop(2)
+            load_hop(3)
+            load_hop(4)
+            load_hop(5)
+
+            nc.scalar.activation(out=warm[:], in_=warm[:], func=EXP)
+
+            for g in range(PASSES):
+                widen(0, g, g + 1)
+            turn_hop(0)
+            widen(1)
+            turn_right(0)
+            turn_hop(1)
+            widen(2)
+            quantize_right(0)
+            turn_right(1)
+
+            quantize_right(1)
+            nc.scalar.activation(out=winv_bc[:], in_=field_bc[:], func=EXP, scale=-1.0)
+            quantize_hop(0)
+            for q in range(6):
+                mult_c(2 * q)
+                mult_c(2 * q + 1)
+                if q == 0:
+                    widen(3)
+                empty_c(2 * q)
+                if q == 0:
+                    quantize_hop(1)
+
+                empty_c(2 * q + 1)
+                if q < 3:
+                    interleave_left(q, S)
+                if q == 2:
+                    nc.scalar.activation(out=w_bc[:], in_=field_bc[:], func=EXP)
+                if q in (2, 3, 4):
+                    quantize_left(q - 2)
+                quantize_c(q)
+            for i in range(TILES + 1):
+                if i + 4 < TILES:
+                    widen(i + 4)
+                if i < TILES:
+                    mult_a(i)
+                if i + 2 < TILES:
+                    turn_hop(i + 2)
+                if i < TILES:
+                    empty_a(i)
+                if i > 0:
+                    finish(i - 1, (S, V, S) if i > 9 else (S, S, S))
+                if i + 2 < TILES:
+                    quantize_hop(i + 2)
+                if i < TILES:
+                    quantize_a(i)

@@ -39,7 +39,11 @@ def tile_wrap_occupied_green_s11_kernel(tc, hop_bytes, hop_scale, left, right, h
         ident = keep.tile([P, P], F32)
         warm = keep.tile([P, 1], F32)
         scale_bc = keep.tile([P, SITES], F32)
-        field_bc = keep.tile([P, SITES], BF16)
+        scale_cols = keep.tile([P, PASSES, PACK], F32)
+        field_cols = keep.tile([P, PASSES, PACK], BF16)
+        w_cols = keep.tile([P, PASSES, PACK], F32)
+        winv_cols = keep.tile([P, PASSES, PACK], F32)
+        zeros = keep.tile([P, N_OUT], BF16)
         w_bc = keep.tile([P, SITES], F32)
         winv_bc = keep.tile([P, SITES], F32)
         right_rows = keep.tile([P, PACK, SITES], BF16)
@@ -63,9 +67,22 @@ def tile_wrap_occupied_green_s11_kernel(tc, hop_bytes, hop_scale, left, right, h
             nc.sync.dma_start(out=hop_tile[:], in_=hop_view[c])
             hop_raw[c] = hop_tile
 
-        def load_scale(g):
-            k = slice(K_PASS * g, K_PASS * (g + 1))
-            nc.sync.dma_start(out=scale_bc[:, k], in_=hop_scale[:, k].rearrange("o k -> (o k)").partition_broadcast(P))
+        def load_columns(cols, row):
+            nc.sync.dma_start(out=cols[:], in_=row.rearrange("(g n q) -> n g q", n=P, q=PACK))
+
+        def spread(cols, g, row_bc):
+            bank = psum.tile([P, PACK, P], F32, name="res", bufs=3)
+            for q in range(PACK):
+                nc.tensor.transpose(bank[:, q, :], cols[:, g, q : q + 1].to_broadcast([P, P]), ident[:])
+            nc.scalar.copy(
+                out=row_bc[:, K_PASS * g : K_PASS * (g + 1)].rearrange("p (n q) -> p n q", q=PACK),
+                in_=bank[:].rearrange("p q n -> p n q"),
+            )
+
+        def keep_warm(n):
+            bank = psum.tile([P, N_OUT], F32, name="res", bufs=3)
+            for x in range(n):
+                nc.tensor.matmul(bank[:], zeros[:, 0:P], zeros[:], start=True, stop=True)
 
         def load_left(g):
             left_tile = keep.tile([P, PACK, ORB], BF16, name=f"left_rows{g}")
@@ -79,7 +96,7 @@ def tile_wrap_occupied_green_s11_kernel(tc, hop_bytes, hop_scale, left, right, h
 
         def widen(i, g0=0, g1=PASSES):
             if g0 == 0:
-                bf_tile = work.tile([P, SITES], BF16, name="hop_bf", bufs=3)
+                bf_tile = work.tile([P, SITES], BF16, name="hop_bf", bufs=4)
                 hop_bf[i] = bf_tile
             k = slice(K_PASS * g0, K_PASS * g1)
             nc.vector.tensor_tensor(out=hop_bf[i][:, k], in0=hop_raw[i // 2][:, i % 2, k].bitcast(FP8), in1=scale_bc[:, k], op=MULT)
@@ -98,7 +115,7 @@ def tile_wrap_occupied_green_s11_kernel(tc, hop_bytes, hop_scale, left, right, h
                 )
 
         def turn_hop(i):
-            grouped = work.tile([P, PASSES, K_PASS], BF16, name="hop_grouped", align_bytes=64, bufs=3)
+            grouped = work.tile([P, PASSES, K_PASS], BF16, name="hop_grouped", align_bytes=64, bufs=4)
             hop_grouped[i] = grouped
             turn(lambda g: hop_bf[i][:, K_PASS * g : K_PASS * (g + 1)].bitcast(F32), grouped, PASSES, S)
 
@@ -230,19 +247,22 @@ def tile_wrap_occupied_green_s11_kernel(tc, hop_bytes, hop_scale, left, right, h
                     stop=True,
                 )
                 copies[q](out=result[:, cols], in_=bank[:])
-            nc.sync.dma_start(out=out_view[i // 2, :, i % 2, :], in_=result[:])
+                if i >= TILES - 2:
+                    nc.sync.dma_start(out=out_view[i // 2, :, i % 2, cols], in_=result[:, cols])
+            if i < TILES - 2:
+                nc.sync.dma_start(out=out_view[i // 2, :, i % 2, :], in_=result[:])
 
         S = nc.scalar.copy
         V = nc.vector.tensor_copy
 
         with tc.manual_schedule():
+            nc.vector.memset(zeros[:].bitcast(U32), 0)
             nc.gpsimd.memset(warm[:], 0.0)
-            nc.gpsimd.memset(hinv_sc[:].rearrange("p g n -> p (g n)").bitcast(U32), 0)
             make_identity(nc, ident[:])
-            load_scale(0)
+            nc.vector.memset(hinv_sc[:].rearrange("p g n -> p (g n)").bitcast(U32), 0)
+            load_columns(scale_cols, hop_scale.rearrange("o k -> (o k)"))
             load_hop(0)
-            load_scale(1)
-            load_scale(2)
+            load_columns(field_cols, field)
             load_right(0)
             load_hop(1)
             load_right(1)
@@ -251,7 +271,6 @@ def tile_wrap_occupied_green_s11_kernel(tc, hop_bytes, hop_scale, left, right, h
                     out=hinv_sc[32 * q : 32 * q + 4, :, :].bitcast(I32),
                     in_=hinv_scales[:, 4 * q : 4 * q + 4, :].rearrange("g q n -> q g n").bitcast(I32),
                 )
-            nc.sync.dma_start(out=field_bc[:], in_=field.partition_broadcast(P))
             load_hinv(0)
             load_left(0)
             load_hinv(1)
@@ -264,43 +283,60 @@ def tile_wrap_occupied_green_s11_kernel(tc, hop_bytes, hop_scale, left, right, h
 
             nc.scalar.activation(out=warm[:], in_=warm[:], func=EXP)
 
+            keep_warm(4)
             for g in range(PASSES):
+                spread(scale_cols, g, scale_bc)
                 widen(0, g, g + 1)
+            nc.scalar.activation(out=winv_cols[:], in_=field_cols[:], func=EXP, scale=-1.0)
+            nc.scalar.activation(out=w_cols[:], in_=field_cols[:], func=EXP)
+            keep_warm(2)
             turn_hop(0)
             widen(1)
+
+            keep_warm(2)
             turn_right(0)
+            keep_warm(2)
             turn_hop(1)
             widen(2)
             quantize_right(0)
             turn_right(1)
-
             quantize_right(1)
-            nc.scalar.activation(out=winv_bc[:], in_=field_bc[:], func=EXP, scale=-1.0)
+            for g in range(PASSES):
+                spread(winv_cols, g, winv_bc)
+            keep_warm(2)
             quantize_hop(0)
+            H = {"w":{3:0},"t":{2:5},"q":{1:0},"li":{0:0,1:1,2:2},"w_bc":3,"lq":{0:2,1:3,2:4}}
             for q in range(6):
                 mult_c(2 * q)
                 mult_c(2 * q + 1)
-                if q == 0:
-                    widen(3)
+                for x, at in H["w"].items():
+                    if at == q:
+                        widen(x)
                 empty_c(2 * q)
-                if q == 0:
-                    quantize_hop(1)
-
+                for x, at in H["q"].items():
+                    if at == q:
+                        quantize_hop(x)
+                for x, at in H["t"].items():
+                    if at == q:
+                        turn_hop(x)
                 empty_c(2 * q + 1)
-                if q < 3:
-                    interleave_left(q, S)
-                if q == 2:
-                    nc.scalar.activation(out=w_bc[:], in_=field_bc[:], func=EXP)
-                if q in (2, 3, 4):
-                    quantize_left(q - 2)
+                for x, at in H["li"].items():
+                    if at == q:
+                        interleave_left(x, S)
+                if q == H["w_bc"]:
+                    for g in range(PASSES):
+                        spread(w_cols, g, w_bc)
+                for x, at in H["lq"].items():
+                    if at == q:
+                        quantize_left(x)
                 quantize_c(q)
             for i in range(TILES + 1):
                 if i + 4 < TILES:
                     widen(i + 4)
                 if i < TILES:
                     mult_a(i)
-                if i + 2 < TILES:
-                    turn_hop(i + 2)
+                if i + 3 < TILES:
+                    turn_hop(i + 3)
                 if i < TILES:
                     empty_a(i)
                 if i > 0:

from contextlib import ExitStack

import concourse.mybir as mybir
from concourse.masks import make_identity

SITES, ORB = 1536, 512

F32 = mybir.dt.float32
BF16 = mybir.dt.bfloat16
U32 = mybir.dt.uint32
I32 = mybir.dt.int32
U8 = mybir.dt.uint8
FP8 = mybir.dt.float8_e4m3fn
E4M3X4 = mybir.dt.float8_e4m3fn_x4
E2M1X4 = mybir.dt.float4_e2m1fn_x4
MULT = mybir.AluOpType.mult
EXP = mybir.ActivationFunctionType.Exp

P = 128
PACK = 4
K_PASS = P * PACK
PASSES = SITES // K_PASS
PAIRS = SITES // (2 * P)
TILES = SITES // P
N_OUT = 512

FLOPS = 3 * 2 * SITES * SITES * ORB


def tile_wrap_occupied_green_s11_kernel(tc, hop_bytes, hop_scale, left, right, hinv_words, hinv_scales, field, out):
    nc = tc.nc

    with ExitStack() as ctx:
        keep = ctx.enter_context(tc.tile_pool(name="keep", bufs=1))
        work = ctx.enter_context(tc.tile_pool(name="work", bufs=2))
        results = ctx.enter_context(tc.tile_pool(name="results", bufs=6))
        psum = ctx.enter_context(tc.psum_pool(name="psum", bufs=1))

        ident = keep.tile([P, P], F32)
        warm = keep.tile([P, 1], F32)
        scale_bc = keep.tile([P, SITES], F32)
        scale_cols = keep.tile([P, PASSES, PACK], F32)
        field_cols = keep.tile([P, PASSES, PACK], BF16)
        w_cols = keep.tile([P, PASSES, PACK], F32)
        winv_cols = keep.tile([P, PASSES, PACK], F32)
        zeros = keep.tile([P, N_OUT], BF16)
        w_bc = keep.tile([P, SITES], F32)
        winv_bc = keep.tile([P, SITES], F32)
        right_rows = keep.tile([P, PACK, SITES], BF16)
        hinv_codes = keep.tile([P, PASSES, 2 * SITES], U8, align_bytes=64)
        hinv_sc = keep.tile([P, PASSES, SITES], U8, align_bytes=64)
        right_codes = keep.tile([P, 2, PASSES, 2 * P], U32, align_bytes=64)
        right_sc = keep.tile([P, 2, PASSES, 2 * P], U8, align_bytes=64)
        left_codes = keep.tile([P, PASSES, ORB], U32, align_bytes=64)
        left_sc = keep.tile([P, PASSES, ORB], U8, align_bytes=64)
        c_codes = keep.tile([P, SITES], U32, align_bytes=64)
        c_sc = keep.tile([P, SITES], U8, align_bytes=64)

        hop_raw, left_rows = {}, {}
        hop_view = hop_bytes.rearrange("(c p s) k -> c p s k", p=P, s=2)
        left_view = left.rearrange("(g p j) r -> g p j r", p=P, j=PACK)
        right_view = right.rearrange("(m t) k -> m t k", t=PACK)
        out_view = out.rearrange("(c p s) j -> c p s j", p=P, s=2)

        def load_hop(c):
            hop_tile = keep.tile([P, 2, SITES], U8, name=f"hop_raw{c}")
            nc.sync.dma_start(out=hop_tile[:], in_=hop_view[c])
            hop_raw[c] = hop_tile

        def load_columns(cols, row):
            nc.sync.dma_start(out=cols[:], in_=row.rearrange("(g n q) -> n g q", n=P, q=PACK))

        def spread(cols, g, row_bc):
            bank = psum.tile([P, PACK, P], F32, name="res", bufs=3)
            for q in range(PACK):
                nc.tensor.transpose(bank[:, q, :], cols[:, g, q : q + 1].to_broadcast([P, P]), ident[:])
            nc.scalar.copy(
                out=row_bc[:, K_PASS * g : K_PASS * (g + 1)].rearrange("p (n q) -> p n q", q=PACK),
                in_=bank[:].rearrange("p q n -> p n q"),
            )

        def keep_warm(n):
            bank = psum.tile([P, N_OUT], F32, name="res", bufs=3)
            for x in range(n):
                nc.tensor.matmul(bank[:], zeros[:, 0:P], zeros[:], start=True, stop=True)

        def load_left(g):
            left_tile = keep.tile([P, PACK, ORB], BF16, name=f"left_rows{g}")
            nc.sync.dma_start(out=left_tile[:], in_=left_view[g])
            left_rows[g] = left_tile

        def load_right(h):
            nc.sync.dma_start(out=right_rows[:, 2 * h : 2 * h + 2, :], in_=right_view[:, 2 * h : 2 * h + 2, :])

        hop_bf, hop_grouped, hop_codes, hop_sc = {}, {}, {}, {}

        def widen(i, g0=0, g1=PASSES):
            if g0 == 0:
                bf_tile = work.tile([P, SITES], BF16, name="hop_bf", bufs=4)
                hop_bf[i] = bf_tile
            k = slice(K_PASS * g0, K_PASS * g1)
            nc.vector.tensor_tensor(out=hop_bf[i][:, k], in0=hop_raw[i // 2][:, i % 2, k].bitcast(FP8), in1=scale_bc[:, k], op=MULT)

        def turn(rows_of_slot, grouped, slots, copy):
            for b in range(0, slots, 2):
                n = min(2, slots - b)
                bank = psum.tile([P, 2, 2, P], F32, name="turned", bufs=3)
                for l in range(n):
                    words = rows_of_slot(b + l)
                    for u in range(2):
                        nc.tensor.transpose(bank[:, l, u, :], words[:, u : 2 * P : 2], ident[:])
                copy(
                    out=grouped[:, b : b + n, :].bitcast(F32).rearrange("p l (r u) -> p l r u", u=2),
                    in_=bank[:, 0:n, :, :].rearrange("p l u r -> p l r u"),
                )

        def turn_hop(i):
            grouped = work.tile([P, PASSES, K_PASS], BF16, name="hop_grouped", align_bytes=64, bufs=4)
            hop_grouped[i] = grouped
            turn(lambda g: hop_bf[i][:, K_PASS * g : K_PASS * (g + 1)].bitcast(F32), grouped, PASSES, S)

        def quantize_slots(grouped, codes, sc, spans):
            flat = grouped[:].rearrange("p l k -> p (l k)")
            for a, b in spans:
                nc.vector.quantize_mx(out=codes[:, a // 4 : b // 4].bitcast(E4M3X4), scales=sc[:, a // 4 : b // 4], in_=flat[:, a:b])

        def quantize_hop(i):
            code_tile = keep.tile([P, PASSES * P], U32, name=f"hop_codes{i}", align_bytes=64)
            sc_tile = keep.tile([P, PASSES * P], U8, name=f"hop_sc{i}", align_bytes=64)
            hop_codes[i], hop_sc[i] = code_tile, sc_tile
            quantize_slots(hop_grouped[i], code_tile, sc_tile, ((0, 1024), (1024, 1536)))

        right_grouped = {}

        def turn_right(h):
            grouped = work.tile([P, 2 * PASSES, K_PASS], BF16, name="right_grouped", align_bytes=64)
            right_grouped[h] = grouped
            turn(lambda i: right_rows[:, 2 * h + i % 2, K_PASS * (i // 2) : K_PASS * (i // 2 + 1)].bitcast(F32), grouped, 2 * PASSES, S)

        def quantize_right(h):
            quantize_slots(
                right_grouped[h],
                right_codes[:, h, :, :].rearrange("p g m -> p (g m)"),
                right_sc[:, h, :, :].rearrange("p g m -> p (g m)"),
                ((0, 2048), (2048, 3072)),
            )

        def load_hinv(h):
            cols = slice(SITES * h, SITES * (h + 1))
            nc.sync.dma_start(out=hinv_codes[:, :, cols], in_=hinv_words[:, :, cols].rearrange("g p n -> p g n"))

        left_grouped = {}

        def interleave_left(g, engine_copy):
            grouped = work.tile([P, ORB * PACK], BF16, name="left_grouped", align_bytes=64)
            left_grouped[g] = grouped
            engine_copy(
                out=grouped[:].rearrange("p (t m j) -> p t m j", t=PACK, j=PACK),
                in_=left_rows[g][:].rearrange("p j (m t) -> p t m j", t=PACK),
            )

        def quantize_left(g):
            nc.vector.quantize_mx(out=left_codes[:, g, :].bitcast(E4M3X4), scales=left_sc[:, g, :], in_=left_grouped[g][:])

        c_acc, c_grouped, a_acc, a_grouped, a_codes, a_sc = {}, {}, {}, {}, {}, {}

        def mult_c(n):
            acc = psum.tile([P, PACK, P], F32, name="acc", bufs=2)
            c_acc[n] = acc
            for t in range(PACK):
                for g in range(PASSES):
                    m = P * (t % 2)
                    nc.tensor.matmul_mx(
                        out=acc[:, t, :],
                        lhsT=right_codes[:, t // 2, g, m : m + P].bitcast(E4M3X4),
                        lhsT_scale=right_sc[:, t // 2, g, m : m + P],
                        rhs=hinv_codes[:, g, 2 * P * n : 2 * P * (n + 1)].bitcast(E2M1X4),
                        rhs_scale=hinv_sc[:, g, P * n : P * (n + 1)],
                        start=(g == 0),
                        stop=(g == PASSES - 1),
                    )

        def empty_c(n):
            if n % 2 == 0:
                grouped = work.tile([P, 2, P, PACK], BF16, name="c_grouped", align_bytes=64)
                c_grouped[n // 2] = grouped
            nc.vector.tensor_tensor(
                out=c_grouped[n // 2][:, n % 2, :, :],
                in0=c_acc[n][:].rearrange("p t n -> p n t"),
                in1=winv_bc[:, P * n : P * (n + 1)].unsqueeze(2).to_broadcast([P, P, PACK]),
                op=MULT,
            )

        def quantize_c(q):
            cols = slice(2 * P * q, 2 * P * (q + 1))
            nc.vector.quantize_mx(
                out=c_codes[:, cols].bitcast(E4M3X4),
                scales=c_sc[:, cols],
                in_=c_grouped[q][:].rearrange("p s n t -> p (s n t)"),
            )

        def mult_a(i):
            acc = psum.tile([P, PACK, P], F32, name="acc", bufs=2)
            a_acc[i] = acc
            for t in range(PACK):
                for g in range(PASSES):
                    cols = slice(g * P, (g + 1) * P)
                    nc.tensor.matmul_mx(
                        out=acc[:, t, :],
                        lhsT=left_codes[:, g, P * t : P * (t + 1)].bitcast(E4M3X4),
                        lhsT_scale=left_sc[:, g, P * t : P * (t + 1)],
                        rhs=hop_codes[i][:, cols].bitcast(E4M3X4),
                        rhs_scale=hop_sc[i][:, cols],
                        start=(g == 0),
                        stop=(g == PASSES - 1),
                    )

        def empty_a(i):
            grouped = work.tile([P, P, PACK], BF16, name="a_grouped", align_bytes=64, bufs=3)
            a_grouped[i] = grouped
            w0 = 2 * P * (i // 2) + i % 2
            nc.vector.tensor_tensor(
                out=grouped[:],
                in0=a_acc[i][:].rearrange("p t n -> p n t"),
                in1=w_bc[:, w0 : w0 + 2 * P - 1 : 2].unsqueeze(2).to_broadcast([P, P, PACK]),
                op=MULT,
            )

        def quantize_a(i):
            code_tile = work.tile([P, P], U32, name="a_codes", align_bytes=64, bufs=3)
            sc_tile = work.tile([P, P], U8, name="a_sc", align_bytes=64, bufs=3)
            a_codes[i], a_sc[i] = code_tile, sc_tile
            nc.vector.quantize_mx(out=code_tile[:].bitcast(E4M3X4), scales=sc_tile[:], in_=a_grouped[i][:].rearrange("p n t -> p (n t)"))

        def finish(i, copies):
            result = results.tile([P, SITES], F32, name="result")
            for q in range(SITES // N_OUT):
                cols = slice(N_OUT * q, N_OUT * (q + 1))
                bank = psum.tile([P, N_OUT], F32, name="res", bufs=3)
                nc.tensor.matmul_mx(
                    out=bank[:],
                    lhsT=a_codes[i][:].bitcast(E4M3X4),
                    lhsT_scale=a_sc[i][:],
                    rhs=c_codes[:, cols].bitcast(E4M3X4),
                    rhs_scale=c_sc[:, cols],
                    start=True,
                    stop=True,
                )
                copies[q](out=result[:, cols], in_=bank[:])
                if i >= TILES - 2:
                    nc.sync.dma_start(out=out_view[i // 2, :, i % 2, cols], in_=result[:, cols])
            if i < TILES - 2:
                nc.sync.dma_start(out=out_view[i // 2, :, i % 2, :], in_=result[:])

        S = nc.scalar.copy
        V = nc.vector.tensor_copy

        with tc.manual_schedule():
            nc.vector.memset(zeros[:].bitcast(U32), 0)
            nc.gpsimd.memset(warm[:], 0.0)
            make_identity(nc, ident[:])
            nc.vector.memset(hinv_sc[:].rearrange("p g n -> p (g n)").bitcast(U32), 0)
            load_columns(scale_cols, hop_scale.rearrange("o k -> (o k)"))
            load_hop(0)
            load_columns(field_cols, field)
            load_right(0)
            load_hop(1)
            load_right(1)
            for q in range(4):
                nc.sync.dma_start(
                    out=hinv_sc[32 * q : 32 * q + 4, :, :].bitcast(I32),
                    in_=hinv_scales[:, 4 * q : 4 * q + 4, :].rearrange("g q n -> q g n").bitcast(I32),
                )
            load_hinv(0)
            load_left(0)
            load_hinv(1)
            load_left(1)
            load_left(2)
            load_hop(2)
            load_hop(3)
            load_hop(4)
            load_hop(5)

            nc.scalar.activation(out=warm[:], in_=warm[:], func=EXP)

            keep_warm(4)
            for g in range(PASSES):
                spread(scale_cols, g, scale_bc)
                widen(0, g, g + 1)
            nc.scalar.activation(out=winv_cols[:], in_=field_cols[:], func=EXP, scale=-1.0)
            nc.scalar.activation(out=w_cols[:], in_=field_cols[:], func=EXP)
            keep_warm(2)
            turn_hop(0)
            widen(1)

            keep_warm(2)
            turn_right(0)
            keep_warm(2)
            turn_hop(1)
            widen(2)
            quantize_right(0)
            turn_right(1)
            quantize_right(1)
            for g in range(PASSES):
                spread(winv_cols, g, winv_bc)
            keep_warm(2)
            quantize_hop(0)
            H = {"w":{3:0},"t":{2:5},"q":{1:0},"li":{0:0,1:1,2:2},"w_bc":3,"lq":{0:2,1:3,2:4}}
            for q in range(6):
                mult_c(2 * q)
                mult_c(2 * q + 1)
                for x, at in H["w"].items():
                    if at == q:
                        widen(x)
                empty_c(2 * q)
                for x, at in H["q"].items():
                    if at == q:
                        quantize_hop(x)
                for x, at in H["t"].items():
                    if at == q:
                        turn_hop(x)
                empty_c(2 * q + 1)
                for x, at in H["li"].items():
                    if at == q:
                        interleave_left(x, S)
                if q == H["w_bc"]:
                    for g in range(PASSES):
                        spread(w_cols, g, w_bc)
                for x, at in H["lq"].items():
                    if at == q:
                        quantize_left(x)
                quantize_c(q)
            for i in range(TILES + 1):
                if i + 4 < TILES:
                    widen(i + 4)
                if i < TILES:
                    mult_a(i)
                if i + 3 < TILES:
                    turn_hop(i + 3)
                if i < TILES:
                    empty_a(i)
                if i > 0:
                    finish(i - 1, (S, V, S) if i > 9 else (S, S, S))
                if i + 2 < TILES:
                    quantize_hop(i + 2)
                if i < TILES:
                    quantize_a(i)
